import numpy as np
import ml_dtypes


def mxq(x, axis, fmt="e4m3"):
    dtype, down = {"e4m3": (ml_dtypes.float8_e4m3fn, 7), "e5m2": (ml_dtypes.float8_e5m2, 14)}[fmt]
    v = np.moveaxis(np.asarray(x, np.float32).astype(ml_dtypes.bfloat16).astype(np.float64), axis, -1)
    blocks = v.reshape(v.shape[:-1] + (-1, 32))
    amax = np.abs(blocks).max(-1, keepdims=True)
    byte = np.maximum(np.where(amax > 0, np.frexp(amax)[1] - 1 + 127, 0) - down, 1)
    scale = np.exp2(byte - 127.0)
    codes = (blocks / scale).astype(np.float32).astype(dtype).astype(np.float64)
    return np.moveaxis((codes * scale).reshape(v.shape), -1, axis)


WIDE = False


def mx_kscale(k):
    if not WIDE:
        return np.ones(k)
    levels = np.array([10, -10, 5, -5, 0])
    if k % 512:
        return np.exp2(np.random.permutation(np.resize(levels, k // 32))).repeat(32)
    a = np.empty((k // 512, 16))
    for p in range(k // 512):
        a[p, :8] = np.random.permutation(np.resize(levels, 8))
        for g in range(8):
            far = levels[np.abs(levels - a[p, g]) >= 10]
            a[p, g + 8] = far[np.random.randint(len(far))]
    return np.exp2(a.ravel()).repeat(32)


def f64(x):
    return np.asarray(x).astype(np.float64)


def striped(idx):
    return np.tile(idx.reshape(-1, 16).T, (8, 1)).astype(np.uint16)


def unstriped(offs):
    return offs[:16].T.reshape(-1).astype(np.int64)


def striped8(idx):
    return np.concatenate([x.reshape(-1, 16).T for x in idx]).astype(np.uint16)


def runs(offs, k):
    lists = np.stack([offs[16 * r : 16 * r + 16].T.reshape(-1) for r in range(8)]).astype(np.int64)
    return lists[np.arange(k) % 512 // 64]


def pack_weight(w):
    k, n = w.shape
    w = f64(np.asarray(w, np.float32).astype(ml_dtypes.bfloat16)).reshape(k // 32, 32, n)
    amax = np.abs(w).max(1)
    byte = np.clip(np.where(amax > 0, np.frexp(amax)[1] - 1 + 127 - 7, 1), 1, 254)
    scaled = (w * np.exp2(127.0 - byte)[:, None, :]).reshape(k, n).astype(np.float32)
    words = np.ascontiguousarray(scaled.reshape(k // 512, 128, 4, n).transpose(0, 1, 3, 2)).astype(ml_dtypes.float8_e4m3fn).view(np.uint8)
    return words, np.ascontiguousarray(byte.astype(np.uint8).reshape(k // 512, 16, n))


def unpack_weight(words, scales):
    g, p, n, _ = words.shape
    vals = np.ascontiguousarray(words).view(ml_dtypes.float8_e4m3fn).astype(np.float64) * np.repeat(np.exp2(scales.astype(np.float64) - 127.0), 8, axis=1)[..., None]
    return vals.transpose(0, 1, 3, 2).reshape(g * 512, n)


def sigmoid(v):
    return 1.0 / (1.0 + np.exp(-np.maximum(v, -700.0)))


K, T, S, N, H = 512, 2048, 512, 512, 512


def setup_inputs():
    n = np.random.standard_normal
    s = mx_kscale(K)[:, None]
    u = mx_kscale(H)
    packed_xT = pack_weight(n((K, T)) * s)
    return {
        "x_words": packed_xT[0],
        "x_scales": packed_xT[1],
        "w1": (n((K, H)) / np.sqrt(K) / s).astype(np.float32),
        "w2": (n((K, H)) / np.sqrt(K) / s).astype(np.float32),
        "w3": (n((K, H)) / np.sqrt(K) / s * u).astype(np.float32),
        "w4": (n((H, N)) / np.sqrt(H) / u[:, None]).astype(np.float32),
        "offs": striped(np.random.permutation(T)[:S]),
        "p1": striped8(np.stack([np.random.permutation(S) for _ in range(8)])),
        "p2": striped8(np.stack([np.random.permutation(S) for _ in range(8)])),
    }


def reference(x_words, x_scales, w1, w2, w3, w4, offs, p1, p2):
    xq = unpack_weight(x_words, x_scales)[:, unstriped(offs)]
    y = mxq(f64(w1), 0, "e4m3").T @ xq
    e = mxq(f64(w2), 0, "e4m3").T @ xq
    s1 = sigmoid(3.0 * (y + e[np.arange(H)[:, None], runs(p1, H)]))
    h = mxq(f64(w3), 0, "e4m3").T @ xq
    s2 = sigmoid(3.0 * (y + e[np.arange(H)[:, None], runs(p2, H)]))
    z = (s1 * (h[np.arange(H)[:, None], runs(p1, H)]) + s2 * (h[np.arange(H)[:, None], runs(p2, H)])) / (s1 + s2 + 0.1)
    return mxq(f64(w4), 0, "e4m3").T @ mxq(z, 0, "e4m3")

@@ -1,0 +1,223 @@
+from contextlib import ExitStack
+
+import concourse.mybir as mybir
+from concourse.masks import make_identity
+
+K, T, S, N, H = 512, 2048, 512, 512, 512
+FLOPS = 2 * (3 * K * H * S + H * N * S)
+
+F32 = mybir.dt.float32
+BF16 = mybir.dt.bfloat16
+I32 = mybir.dt.int32
+U32 = mybir.dt.uint32
+U16 = mybir.dt.uint16
+U8 = mybir.dt.uint8
+FP8X4 = mybir.dt.float8_e4m3fn_x4
+ACT = mybir.ActivationFunctionType
+ALU = mybir.AluOpType
+
+P = 128
+PACK = 4
+TILES = H // P
+RUNS = 8
+PER_RUN = P // RUNS
+CHUNKS = ((0, 2), (2, 3), (3, 4))
+
+
+def tile_picked_ggnorm_none_p_kernel(tc, x_words, x_scales, w1, w2, w3, w4, offs, p1, p2, out):
+    nc = tc.nc
+    with ExitStack() as ctx:
+        sb = ctx.enter_context(tc.tile_pool(name="sb", bufs=1))
+        psum = ctx.enter_context(tc.psum_pool(name="psum", bufs=1))
+
+        def tile(name, shape, dtype):
+            return sb.tile(shape, dtype, name=name, align_bytes=64)
+
+        def bank(b, name):
+            return psum.tile([P, 512], F32, name=name, tag="bank%d" % b)
+
+        offs_sb = tile("offs_sb", [P, S // 16], U16)
+        lists = [tile("p1_sb", [P, S // 16], U16), tile("p2_sb", [P, S // 16], U16)]
+        xw_all = tile("xw_all", [P, T], I32)
+        xs_all = tile("xs_all", [P, T], U8)
+        xw = tile("xw", [P, S], U32)
+        xs = tile("xs", [P, S], U8)
+        w2_raw = tile("w2_raw", [P, PACK, H], F32)
+        w1_raw = [tile("w1_raw%d" % a, [P, PACK, H // 2], F32) for a in range(2)]
+        w3_raw = tile("w3_raw", [P, PACK, H], F32)
+        w4_raw = tile("w4_raw", [P, PACK, N], F32)
+        ident = tile("ident", [P, P], F32)
+        warm = tile("warm", [P, 8], F32)
+
+        def rows(w):
+            return w.rearrange("(p j) c -> p j c", j=PACK)
+
+        nc.vector.memset(xs_all[:].bitcast(I32), 0)
+        nc.vector.memset(warm[:, 0:1], 0.0)
+        nc.scalar.activation(warm[:, 1:2], warm[:, 0:1], ACT.Sigmoid)
+        nc.sync.dma_start(w2_raw[:], rows(w2))
+        nc.sync.dma_start(offs_sb[:], offs)
+        for q in range(4):
+            nc.scalar.dma_start(xs_all[32 * q : 32 * q + 4, :].bitcast(I32), x_scales[0, 4 * q : 4 * q + 4, :].bitcast(I32))
+        nc.sync.dma_start(xw_all[:], x_words[0].rearrange("p c r -> p (c r)").bitcast(I32))
+        nc.sync.dma_start(lists[0][:], p1)
+        nc.sync.dma_start(lists[1][:], p2)
+        for a in range(2):
+            nc.sync.dma_start(w1_raw[a][:], rows(w1)[:, :, a * (H // 2) : (a + 1) * (H // 2)])
+        nc.sync.dma_start(w3_raw[:], rows(w3))
+        nc.sync.dma_start(w4_raw[:], rows(w4))
+
+        make_identity(nc, ident[:])
+        e_sb = [tile("e_sb%d" % t, [P, 2 * S], F32) for t in range(TILES)]
+        for t in range(TILES):
+            nc.gpsimd.memset(e_sb[t][:, S:], 0.0)
+        y_sb = [tile("y_sb%d" % t, [P, S], F32) for t in range(TILES)]
+        h_sb = [tile("h_sb%d" % t, [P, S], F32) for t in range(TILES)]
+        u_sb = [[tile("u_sb%d_%d" % (t, l), [P, S], F32) for l in range(2)] for t in range(TILES)]
+        s_sb = [[tile("s_sb%d_%d" % (t, l), [P, S], F32) for l in range(2)] for t in range(TILES)]
+
+        def weight_tiles(name):
+            return [
+                (tile("%s_bf%d" % (name, t), [P, P * PACK], BF16), tile("%s_codes%d" % (name, t), [P, P], U32), tile("%s_scales%d" % (name, t), [P, P], U8))
+                for t in range(TILES)
+            ]
+
+        q1, q2, q3, q4 = weight_tiles("w1"), weight_tiles("w2"), weight_tiles("w3"), weight_tiles("w4")
+
+        def deal(copy, raw, staged, t, first_run, runs):
+            src = raw[:].rearrange("p j (g t r i) -> p t g r j i", t=TILES, r=PER_RUN // 4, i=4)[:, t]
+            dst = staged[:].rearrange("p (g r i j) -> p g r j i", g=RUNS, i=4, j=PACK)[:, first_run : first_run + runs]
+            copy(dst, src)
+
+        def weave(copy, raw, staged, t):
+            src = raw[:, :, t * P : (t + 1) * P].rearrange("p j (c i) -> p c j i", i=4)
+            dst = staged[:].rearrange("p (c i j) -> p c j i", i=4, j=PACK)
+            copy(dst, src)
+
+        def quantize(tiles):
+            staged, codes, scales = tiles
+            nc.vector.quantize_mx(out=codes[:].bitcast(FP8X4), scales=scales[:], in_=staged[:])
+
+        def product(acc, weights, codes, scales):
+            nc.tensor.matmul_mx(out=acc, lhsT=weights[1][:].bitcast(FP8X4), lhsT_scale=weights[2][:], rhs=codes.bitcast(FP8X4), rhs_scale=scales, start=True, stop=True)
+
+        def first_layer(weights, t, dst, name):
+            acc = bank(t, "%s_acc%d" % (name, t))
+            product(acc[:], weights[t], xw[:], xs[:])
+            return lambda: nc.scalar.copy(dst, acc[:])
+
+        def add_turned(acc, t, pair):
+            dst = acc[:].rearrange("j (g t r) -> j t g r", t=TILES, r=PER_RUN)[:, t]
+            for l in range(2):
+                nc.tensor.matmul(dst, pair[l], ident[:], start=(l == 0), stop=(l == 1), is_transpose=True)
+
+        nc.vector.tensor_copy(xs[:], xs_all[:].indirect(offs_sb[:]))
+        for t in range(TILES + 1):
+            if t < TILES:
+                deal(nc.vector.tensor_copy, w2_raw, q2[t][0], t, 0, RUNS)
+            if t > 0:
+                quantize(q2[t - 1])
+        nc.vector.tensor_copy(xw[:], xw_all[:].bitcast(U32).indirect(offs_sb[:]))
+        e_out = [first_layer(q2, t, e_sb[t][:, :S], "e") for t in range(TILES)]
+        for t in range(TILES - 1):
+            e_out[t]()
+        for t in range(TILES):
+            deal(nc.vector.tensor_copy, w1_raw[0], q1[t][0], t, 0, RUNS // 2)
+        for t in range(TILES + 1):
+            if t < TILES:
+                deal(nc.vector.tensor_copy, w1_raw[1], q1[t][0], t, RUNS // 2, RUNS // 2)
+            if t > 0:
+                quantize(q1[t - 1])
+        first_layer(q1, 0, y_sb[0][:], "y")()
+        e_out[TILES - 1]()
+        first_layer(q1, 1, y_sb[1][:], "y")()
+
+        den = [bank(4 + jt, "den%d" % jt) for jt in range(TILES)]
+        for t in range(TILES):
+            for l in range(2):
+                nc.vector.tensor_tensor(u_sb[t][l][:], e_sb[t][:].indirect(lists[l][:]), y_sb[t][:], ALU.add)
+                nc.scalar.activation(s_sb[t][l][:], u_sb[t][l][:], ACT.Sigmoid, scale=3.0)
+                if l == 0:
+                    deal(nc.scalar.copy, w3_raw, q3[t][0], t, 0, RUNS)
+            if t + 2 < TILES:
+                first_layer(q1, t + 2, y_sb[t + 2][:], "y")()
+            quantize(q3[t])
+            for jt in range(TILES):
+                add_turned(den[jt], t, [s_sb[t][l][:, jt * P : (jt + 1) * P] for l in range(2)])
+            if t >= 1:
+                first_layer(q3, t - 1, h_sb[t - 1][:], "h")()
+        first_layer(q3, TILES - 1, h_sb[TILES - 1][:], "h")()
+
+        root = [tile("root%d" % jt, [P, H], F32) for jt in range(TILES)]
+        recip = [tile("recip%d" % jt, [P, H], F32) for jt in range(TILES)]
+
+        def paired(ap):
+            return ap.rearrange("j (p u e) -> j u p e", u=2, e=2)
+
+        def flat(ap):
+            return ap.rearrange("j (u p e) -> j u p e", u=2, e=2)
+
+        def reciprocal(jt):
+            nc.scalar.activation(flat(root[jt][:]), paired(den[jt][:]), ACT.Abs_reciprocal_sqrt, bias=0.1)
+            nc.scalar.activation(recip[jt][:], root[jt][:], ACT.Square)
+
+        num = [None] * TILES
+        zq = [(tile("z_bf%d" % jt, [P, P * PACK], BF16), tile("z_codes%d" % jt, [P, P], U32), tile("z_scales%d" % jt, [P, P], U8)) for jt in range(TILES)]
+        zt = [tile("zt%d" % jt, [P, H], BF16) for jt in range(TILES)]
+        staged_out = [tile("staged_out%d" % c, [P, TILES, (b - a) * P], F32) for c, (a, b) in enumerate(CHUNKS)]
+
+        def gather_chunk(c):
+            a, b = CHUNKS[c]
+            for jt in range(a, b):
+                num[jt] = bank(jt, "num%d" % jt)
+            for t in range(TILES):
+                pair = [tile("n_sb%d_%d_%d" % (c, t, l), [P, (b - a) * P], F32) for l in range(2)]
+                for l in range(2):
+                    nc.vector.tensor_tensor(pair[l][:], h_sb[t][:].indirect(lists[l][:, a * 8 : b * 8]), s_sb[t][l][:, a * P : b * P], ALU.mult)
+                for jt in range(a, b):
+                    add_turned(num[jt], t, [pair[l][:, (jt - a) * P : (jt - a + 1) * P] for l in range(2)])
+
+        def normalise(jt):
+            nc.vector.tensor_tensor(flat(zt[jt][:]), paired(num[jt][:]), flat(recip[jt][:]), ALU.mult)
+            back = bank(4 + jt, "back%d" % jt)
+            words = zt[jt][:].bitcast(F32)
+            for u in range(2):
+                nc.tensor.transpose(back[:, u * P : (u + 1) * P], words[:, u * P : (u + 1) * P], ident[:])
+            nc.scalar.copy(zq[jt][0][:].bitcast(F32).rearrange("p (j u) -> p j u", u=2), back[:, : 2 * P].rearrange("p (u j) -> p j u", u=2))
+
+        def last_layer(c, jt, copies):
+            a, b = CHUNKS[c]
+            quantize(zq[jt])
+            accs = [bank(4 + jt, "out%d_0" % jt), bank(jt, "out%d_1" % jt)]
+            for half in range(2):
+                for m in range(2):
+                    product(accs[half][:, m * P : (m + 1) * P], q4[2 * half + m], zq[jt][1][:], zq[jt][2][:])
+                copies[half](staged_out[c][:, 2 * half : 2 * half + 2, (jt - a) * P : (jt - a + 1) * P], accs[half][:, : 2 * P].rearrange("p (m j) -> p m j", m=2))
+
+        def store(c):
+            a, b = CHUNKS[c]
+            nc.sync.dma_start(out.rearrange("(m p) j -> p m j", p=P)[:, :, a * P : b * P], staged_out[c][:])
+
+        on_scalar = (nc.scalar.copy, nc.scalar.copy)
+        reciprocal(0)
+        reciprocal(1)
+        for t in range(TILES):
+            weave(nc.scalar.copy, w4_raw, q4[t][0], t)
+        gather_chunk(0)
+        gather_chunk(1)
+        normalise(0)
+        normalise(1)
+        reciprocal(2)
+        reciprocal(3)
+        for t in range(TILES):
+            quantize(q4[t])
+        last_layer(0, 0, on_scalar)
+        last_layer(0, 1, on_scalar)
+        store(0)
+        normalise(2)
+        gather_chunk(2)
+        last_layer(1, 2, on_scalar)
+        store(1)
+        normalise(3)
+        last_layer(2, 3, (nc.scalar.copy, nc.vector.tensor_copy))
+        store(2)

@@ -19,9 +19,10 @@ ALU = mybir.AluOpType
 P = 128
 PACK = 4
 TILES = H // P
-RUNS = 8
-PER_RUN = P // RUNS
-CHUNKS = ((0, 2), (2, 3), (3, 4))
+BLOCKS = 16
+PER_BLOCK = P // BLOCKS
+CHUNKS = ((0, 3), (3, 4))
+STORES = ((0, 2), (2, 3), (3, 4))
 
 
 def tile_picked_ggnorm_none_p_kernel(tc, x_words, x_scales, w1, w2, w3, w4, offs, p1, p2, out):
@@ -65,7 +66,8 @@ def tile_picked_ggnorm_none_p_kernel(tc, x_words, x_scales, w1, w2, w3, w4, offs
         for a in range(2):
             nc.sync.dma_start(w1_raw[a][:], rows(w1)[:, :, a * (H // 2) : (a + 1) * (H // 2)])
         nc.sync.dma_start(w3_raw[:], rows(w3))
-        nc.sync.dma_start(w4_raw[:], rows(w4))
+        for t in range(TILES):
+            nc.sync.dma_start(w4_raw[:, t, :], w4.rearrange("(b t r) n -> t b r n", t=TILES, r=PER_BLOCK)[t])
 
         make_identity(nc, ident[:])
         e_sb = [tile("e_sb%d" % t, [P, 2 * S], F32) for t in range(TILES)]
@@ -73,7 +75,7 @@ def tile_picked_ggnorm_none_p_kernel(tc, x_words, x_scales, w1, w2, w3, w4, offs
             nc.gpsimd.memset(e_sb[t][:, S:], 0.0)
         y_sb = [tile("y_sb%d" % t, [P, S], F32) for t in range(TILES)]
         h_sb = [tile("h_sb%d" % t, [P, S], F32) for t in range(TILES)]
-        u_sb = [[tile("u_sb%d_%d" % (t, l), [P, S], F32) for l in range(2)] for t in range(TILES)]
+        u_sb = [tile("u_sb%d" % t, [P, 2, S], F32) for t in range(TILES)]
         s_sb = [[tile("s_sb%d_%d" % (t, l), [P, S], F32) for l in range(2)] for t in range(TILES)]
 
         def weight_tiles(name):
@@ -82,11 +84,17 @@ def tile_picked_ggnorm_none_p_kernel(tc, x_words, x_scales, w1, w2, w3, w4, offs
                 for t in range(TILES)
             ]
 
-        q1, q2, q3, q4 = weight_tiles("w1"), weight_tiles("w2"), weight_tiles("w3"), weight_tiles("w4")
+        q1, q2 = weight_tiles("w1"), weight_tiles("w2")
+        w3_pairs = [(tile("w3_bf%d" % a, [P, 2 * P * PACK], BF16), tile("w3_codes%d" % a, [P, 2 * P], U32), tile("w3_scales%d" % a, [P, 2 * P], U8)) for a in range(TILES // 2)]
+        q3 = [(bf[:, b * P * PACK : (b + 1) * P * PACK], codes[:, b * P : (b + 1) * P], scales[:, b * P : (b + 1) * P]) for bf, codes, scales in w3_pairs for b in range(2)]
+        w4_bf = u_sb[TILES - 1][:].rearrange("p l s -> p (l s)").bitcast(BF16)
+        w4_codes = tile("w4_codes", [P, N], U32)
+        w4_scales = tile("w4_scales", [P, N], U8)
+        q4 = [(w4_bf[:, t * P * PACK : (t + 1) * P * PACK], w4_codes[:, t * P : (t + 1) * P], w4_scales[:, t * P : (t + 1) * P]) for t in range(TILES)]
 
-        def deal(copy, raw, staged, t, first_run, runs):
-            src = raw[:].rearrange("p j (g t r i) -> p t g r j i", t=TILES, r=PER_RUN // 4, i=4)[:, t]
-            dst = staged[:].rearrange("p (g r i j) -> p g r j i", g=RUNS, i=4, j=PACK)[:, first_run : first_run + runs]
+        def deal(copy, raw, staged, t, first_block, blocks):
+            src = raw[:].rearrange("p j (b t r i) -> p t b r j i", t=TILES, r=PER_BLOCK // 4, i=4)[:, t]
+            dst = staged[:].rearrange("p (b r i j) -> p b r j i", b=BLOCKS, i=4, j=PACK)[:, first_block : first_block + blocks]
             copy(dst, src)
 
         def weave(copy, raw, staged, t):
@@ -101,123 +109,179 @@ def tile_picked_ggnorm_none_p_kernel(tc, x_words, x_scales, w1, w2, w3, w4, offs
         def product(acc, weights, codes, scales):
             nc.tensor.matmul_mx(out=acc, lhsT=weights[1][:].bitcast(FP8X4), lhsT_scale=weights[2][:], rhs=codes.bitcast(FP8X4), rhs_scale=scales, start=True, stop=True)
 
-        def first_layer(weights, t, dst, name):
-            acc = bank(t, "%s_acc%d" % (name, t))
+        def first_layer(weights, t, dst, b, name):
+            acc = bank(b, "%s_acc%d" % (name, t))
             product(acc[:], weights[t], xw[:], xs[:])
             return lambda: nc.scalar.copy(dst, acc[:])
 
         def add_turned(acc, t, pair):
-            dst = acc[:].rearrange("j (g t r) -> j t g r", t=TILES, r=PER_RUN)[:, t]
+            dst = acc[:, t * P : (t + 1) * P]
             for l in range(2):
                 nc.tensor.matmul(dst, pair[l], ident[:], start=(l == 0), stop=(l == 1), is_transpose=True)
 
         nc.vector.tensor_copy(xs[:], xs_all[:].indirect(offs_sb[:]))
         for t in range(TILES + 1):
             if t < TILES:
-                deal(nc.vector.tensor_copy, w2_raw, q2[t][0], t, 0, RUNS)
+                deal(nc.vector.tensor_copy, w2_raw, q2[t][0], t, 0, BLOCKS)
             if t > 0:
                 quantize(q2[t - 1])
         nc.vector.tensor_copy(xw[:], xw_all[:].bitcast(U32).indirect(offs_sb[:]))
-        e_out = [first_layer(q2, t, e_sb[t][:, :S], "e") for t in range(TILES)]
-        for t in range(TILES - 1):
-            e_out[t]()
+        for t in range(2):
+            first_layer(q2, t, e_sb[t][:, :S], t, "e")()
         for t in range(TILES):
-            deal(nc.vector.tensor_copy, w1_raw[0], q1[t][0], t, 0, RUNS // 2)
+            deal(nc.vector.tensor_copy, w1_raw[0], q1[t][0], t, 0, BLOCKS // 2)
         for t in range(TILES + 1):
             if t < TILES:
-                deal(nc.vector.tensor_copy, w1_raw[1], q1[t][0], t, RUNS // 2, RUNS // 2)
+                deal(nc.vector.tensor_copy, w1_raw[1], q1[t][0], t, BLOCKS // 2, BLOCKS // 2)
             if t > 0:
                 quantize(q1[t - 1])
-        first_layer(q1, 0, y_sb[0][:], "y")()
-        e_out[TILES - 1]()
-        first_layer(q1, 1, y_sb[1][:], "y")()
+        for half, (b, copy) in enumerate(((4, nc.vector.tensor_copy), (5, nc.scalar.copy))):
+            cols = slice(half * (S // 2), (half + 1) * (S // 2))
+            acc = bank(b, "y_half%d" % half)
+            product(acc[:, : S // 2], q1[0], xw[:, cols], xs[:, cols])
+            copy(y_sb[0][:, cols], acc[:, : S // 2])
+        y_out = {t: first_layer(q1, t, y_sb[t][:], b, "y") for t, b in ((1, 6), (2, 7), (3, 2))}
+        e_out = {t: first_layer(q2, t, e_sb[t][:, :S], b, "e") for t, b in ((2, 4), (3, 5))}
 
-        den = [bank(4 + jt, "den%d" % jt) for jt in range(TILES)]
-        for t in range(TILES):
-            for l in range(2):
-                nc.vector.tensor_tensor(u_sb[t][l][:], e_sb[t][:].indirect(lists[l][:]), y_sb[t][:], ALU.add)
-                nc.scalar.activation(s_sb[t][l][:], u_sb[t][l][:], ACT.Sigmoid, scale=3.0)
-                if l == 0:
-                    deal(nc.scalar.copy, w3_raw, q3[t][0], t, 0, RUNS)
-            if t + 2 < TILES:
-                first_layer(q1, t + 2, y_sb[t + 2][:], "y")()
-            quantize(q3[t])
+        def gate(t, l):
+            nc.vector.tensor_tensor(u_sb[t][:, l, :], e_sb[t][:].indirect(lists[l][:]), y_sb[t][:], ALU.add)
+            nc.scalar.activation(s_sb[t][l][:], u_sb[t][:, l, :], ACT.Sigmoid, scale=3.0)
+
+        def w3_tile(t):
+            deal(nc.scalar.copy, w3_raw, q3[t][0], t, 0, BLOCKS)
+            if t % 2 == 1:
+                quantize(w3_pairs[t // 2])
+
+        def h_tile(t):
+            first_layer(q3, t, h_sb[t][:], t, "h")()
+
+        den = [bank(TILES + jt, "den%d" % jt) for jt in range(TILES)]
+
+        def den_tile(t):
             for jt in range(TILES):
                 add_turned(den[jt], t, [s_sb[t][l][:, jt * P : (jt + 1) * P] for l in range(2)])
-            if t >= 1:
-                first_layer(q3, t - 1, h_sb[t - 1][:], "h")()
-        first_layer(q3, TILES - 1, h_sb[TILES - 1][:], "h")()
 
-        root = [tile("root%d" % jt, [P, H], F32) for jt in range(TILES)]
-        recip = [tile("recip%d" % jt, [P, H], F32) for jt in range(TILES)]
+        y_out[1]()
+        w3_tile(0)
+        e_out[2]()
+        gate(0, 0)
+        y_out[2]()
+        w3_tile(1)
+        gate(0, 1)
+        e_out[3]()
+        gate(1, 0)
+        y_out[3]()
+        w3_tile(2)
+        gate(1, 1)
+        den_tile(0)
+        w3_tile(3)
+        gate(2, 0)
+        den_tile(1)
+        h_tile(0)
+        gate(2, 1)
+        h_tile(1)
+        den_tile(2)
+        gate(3, 0)
+        h_tile(2)
+        gate(3, 1)
+        den_tile(3)
+        h_tile(3)
+
+        root = tile("root", [P, TILES - 1, H], F32)
+        recip = tile("recip", [P, TILES, H], F32)
+        recip_of = [recip[:, 0, :].rearrange("j (u c) -> j u c", u=2), recip[:, 1, :].rearrange("j (u c) -> j u c", u=2), recip[:, 2:, : H // 2]]
+        recip_last = tile("recip_last", [P, H], F32)
+        num_last = tile("num_last", [P, TILES, P], F32)
+        last = TILES - 1
 
         def paired(ap):
-            return ap.rearrange("j (p u e) -> j u p e", u=2, e=2)
+            return ap.rearrange("j (u e p) -> j u p e", u=2, e=2)
 
         def flat(ap):
             return ap.rearrange("j (u p e) -> j u p e", u=2, e=2)
 
-        def reciprocal(jt):
-            nc.scalar.activation(flat(root[jt][:]), paired(den[jt][:]), ACT.Abs_reciprocal_sqrt, bias=0.1)
-            nc.scalar.activation(recip[jt][:], root[jt][:], ACT.Square)
+        def inverse_root(jt):
+            nc.scalar.activation(flat(root[:, jt, :]), paired(den[jt][:]), ACT.Abs_reciprocal_sqrt, bias=0.1)
 
-        num = [None] * TILES
-        zq = [(tile("z_bf%d" % jt, [P, P * PACK], BF16), tile("z_codes%d" % jt, [P, P], U32), tile("z_scales%d" % jt, [P, P], U8)) for jt in range(TILES)]
-        zt = [tile("zt%d" % jt, [P, H], BF16) for jt in range(TILES)]
-        staged_out = [tile("staged_out%d" % c, [P, TILES, (b - a) * P], F32) for c, (a, b) in enumerate(CHUNKS)]
+        zq = [(tile("z_bf%d" % c, [P, (b - a) * P * PACK], BF16), tile("z_codes%d" % c, [P, (b - a) * P], U32), tile("z_scales%d" % c, [P, (b - a) * P], U8)) for c, (a, b) in enumerate(STORES)]
+        zt_pair = tile("zt_pair", [P, 2 * H], BF16)
+        zt = [zt_pair[:, :H], zt_pair[:, H:], zq[0][0][:, :H]]
+        root_last = zt_pair[:].bitcast(F32)
+        staged_out = [tile("staged_out%d" % c, [P, TILES, (b - a) * P], F32) for c, (a, b) in enumerate(STORES)]
+        num = [bank(jt, "num%d" % jt) for jt in range(last)]
 
-        def gather_chunk(c):
-            a, b = CHUNKS[c]
-            for jt in range(a, b):
-                num[jt] = bank(jt, "num%d" % jt)
-            for t in range(TILES):
-                pair = [tile("n_sb%d_%d_%d" % (c, t, l), [P, (b - a) * P], F32) for l in range(2)]
-                for l in range(2):
-                    nc.vector.tensor_tensor(pair[l][:], h_sb[t][:].indirect(lists[l][:, a * 8 : b * 8]), s_sb[t][l][:, a * P : b * P], ALU.mult)
-                for jt in range(a, b):
-                    add_turned(num[jt], t, [pair[l][:, (jt - a) * P : (jt - a + 1) * P] for l in range(2)])
+        def weigh(t, a, b, pair):
+            for l in range(2):
+                nc.vector.tensor_tensor(pair[l], h_sb[t][:].indirect(lists[l][:, a * 8 : b * 8]), s_sb[t][l][:, a * P : b * P], ALU.mult)
 
-        def normalise(jt):
-            nc.vector.tensor_tensor(flat(zt[jt][:]), paired(num[jt][:]), flat(recip[jt][:]), ALU.mult)
-            back = bank(4 + jt, "back%d" % jt)
+        def normalise(jt, c):
+            nc.vector.tensor_tensor(flat(zt[jt][:]), paired(num[jt][:]), recip_of[jt].rearrange("j u (p e) -> j u p e", e=2), ALU.mult)
+            back = bank(TILES + jt, "back%d" % jt)
             words = zt[jt][:].bitcast(F32)
             for u in range(2):
                 nc.tensor.transpose(back[:, u * P : (u + 1) * P], words[:, u * P : (u + 1) * P], ident[:])
-            nc.scalar.copy(zq[jt][0][:].bitcast(F32).rearrange("p (j u) -> p j u", u=2), back[:, : 2 * P].rearrange("p (u j) -> p j u", u=2))
+            first = (jt - STORES[c][0]) * 2 * P
+            nc.scalar.copy(zq[c][0][:].bitcast(F32)[:, first : first + 2 * P].rearrange("p (j u) -> p j u", u=2), back[:, : 2 * P].rearrange("p (u j) -> p j u", u=2))
 
-        def last_layer(c, jt, copies):
-            a, b = CHUNKS[c]
-            quantize(zq[jt])
-            accs = [bank(4 + jt, "out%d_0" % jt), bank(jt, "out%d_1" % jt)]
+        def last_layer(c, banks, copies):
+            a, b = STORES[c]
+            width = (b - a) * P
             for half in range(2):
+                acc = bank(banks[half], "out%d_%d" % (c, half))
                 for m in range(2):
-                    product(accs[half][:, m * P : (m + 1) * P], q4[2 * half + m], zq[jt][1][:], zq[jt][2][:])
-                copies[half](staged_out[c][:, 2 * half : 2 * half + 2, (jt - a) * P : (jt - a + 1) * P], accs[half][:, : 2 * P].rearrange("p (m j) -> p m j", m=2))
+                    product(acc[:, m * width : (m + 1) * width], q4[2 * half + m], zq[c][1][:], zq[c][2][:])
+                copies[half](staged_out[c][:, 2 * half : 2 * half + 2, :], acc[:, : 2 * width].rearrange("p (m j) -> p m j", m=2))
 
-        def store(c):
-            a, b = CHUNKS[c]
-            nc.sync.dma_start(out.rearrange("(m p) j -> p m j", p=P)[:, :, a * P : b * P], staged_out[c][:])
+        def store(c, queue, m0, m1):
+            a, b = STORES[c]
+            queue.dma_start(out.rearrange("(m p) j -> p m j", p=P)[:, m0:m1, a * P : b * P], staged_out[c][:, m0:m1, :])
 
         on_scalar = (nc.scalar.copy, nc.scalar.copy)
-        reciprocal(0)
-        reciprocal(1)
+        for t in range(TILES):
+            wide = tile("n_wide%d" % t, [P, 2, last * P], F32)
+            weigh(t, 0, last, [wide[:, l, :] for l in range(2)])
+            for jt in range(last):
+                add_turned(num[jt], t, [wide[:, l, jt * P : (jt + 1) * P] for l in range(2)])
+
+        inverse_root(0)
+        inverse_root(1)
+        nc.scalar.activation(recip[:, :2, :], root[:, :2, :], ACT.Square)
         for t in range(TILES):
             weave(nc.scalar.copy, w4_raw, q4[t][0], t)
-        gather_chunk(0)
-        gather_chunk(1)
-        normalise(0)
-        normalise(1)
-        reciprocal(2)
-        reciprocal(3)
+        inverse_root(2)
+        nc.scalar.activation(recip_of[2], root[:, 2, :].rearrange("j (u c) -> j u c", u=2), ACT.Square)
+        narrow = [recip[:, :, l * P : (l + 1) * P] for l in range(2)]
+        normalise(0, 0)
+        weigh(0, last, TILES, [narrow[l][:, 0, :] for l in range(2)])
+        normalise(1, 0)
+        weigh(1, last, TILES, [narrow[l][:, 1, :] for l in range(2)])
+        nc.scalar.activation(root_last, den[last][:], ACT.Abs_reciprocal_sqrt, bias=0.1)
+        root_back = bank(last, "root_back")
         for t in range(TILES):
-            quantize(q4[t])
-        last_layer(0, 0, on_scalar)
-        last_layer(0, 1, on_scalar)
-        store(0)
-        normalise(2)
-        gather_chunk(2)
-        last_layer(1, 2, on_scalar)
-        store(1)
-        normalise(3)
-        last_layer(2, 3, (nc.scalar.copy, nc.vector.tensor_copy))
-        store(2)
+            nc.tensor.transpose(root_back[:, t * P : (t + 1) * P], root_last[:, t * P : (t + 1) * P], ident[:])
+        quantize((w4_bf, w4_codes, w4_scales))
+        quantize(zq[0])
+        last_layer(0, (TILES, TILES + 1), on_scalar)
+        store(0, nc.sync, 0, TILES)
+        nc.scalar.activation(recip_last[:].rearrange("p (j t) -> p j t", t=TILES), root_back[:].rearrange("p (t j) -> p j t", t=TILES), ACT.Square)
+        normalise(2, 1)
+        weigh(2, last, TILES, [narrow[l][:, 2, :] for l in range(2)])
+        weigh(3, last, TILES, [narrow[l][:, 3, :] for l in range(2)])
+        quantize(zq[1])
+        last_layer(1, (0, 1), on_scalar)
+        store(1, nc.sync, 0, TILES)
+        halves = [slice(a * P // 2, (a + 1) * P // 2) for a in range(2)]
+        for cols in halves:
+            nc.vector.tensor_tensor(num_last[:, :, cols], narrow[0][:, :, cols], narrow[1][:, :, cols], ALU.add)
+        for cols in halves:
+            nc.vector.tensor_tensor(
+                zq[2][0][:].rearrange("p (j t) -> p j t", t=TILES)[:, cols],
+                num_last[:].rearrange("p t j -> p j t")[:, cols],
+                recip_last[:].rearrange("p (j t) -> p j t", t=TILES)[:, cols],
+                ALU.mult,
+            )
+        for cols in halves:
+            quantize((zq[2][0][:, cols.start * PACK : cols.stop * PACK], zq[2][1][:, cols], zq[2][2][:, cols]))
+        last_layer(2, (2, last), (nc.vector.tensor_copy, nc.scalar.copy))
+        store(2, nc.sync, 0, 2)
+        store(2, nc.scalar, 2, TILES)

@@ -53,18 +53,18 @@ def tile_picked_ggnorm_none_p_kernel(tc, x_words, x_scales, w1, w2, w3, w4, offs
         def rows(w):
             return w.rearrange("(p j) c -> p j c", j=PACK)
 
-        nc.vector.memset(xs_all[:].bitcast(I32), 0)
+        nc.gpsimd.memset(xs_all[:].bitcast(I32), 0)
         nc.vector.memset(warm[:, 0:1], 0.0)
         nc.scalar.activation(warm[:, 1:2], warm[:, 0:1], ACT.Sigmoid)
         nc.sync.dma_start(w2_raw[:], rows(w2))
         nc.sync.dma_start(offs_sb[:], offs)
         for q in range(4):
-            nc.scalar.dma_start(xs_all[32 * q : 32 * q + 4, :].bitcast(I32), x_scales[0, 4 * q : 4 * q + 4, :].bitcast(I32))
+            nc.sync.dma_start(xs_all[32 * q : 32 * q + 4, :].bitcast(I32), x_scales[0, 4 * q : 4 * q + 4, :].bitcast(I32))
         nc.sync.dma_start(xw_all[:], x_words[0].rearrange("p c r -> p (c r)").bitcast(I32))
-        nc.sync.dma_start(lists[0][:], p1)
-        nc.sync.dma_start(lists[1][:], p2)
         for a in range(2):
             nc.sync.dma_start(w1_raw[a][:], rows(w1)[:, :, a * (H // 2) : (a + 1) * (H // 2)])
+        nc.sync.dma_start(lists[0][:], p1)
+        nc.sync.dma_start(lists[1][:], p2)
         nc.sync.dma_start(w3_raw[:], rows(w3))
         for t in range(TILES):
             nc.sync.dma_start(w4_raw[:, t, :], w4.rearrange("(b t r) n -> t b r n", t=TILES, r=PER_BLOCK)[t])
@@ -144,7 +144,10 @@ def tile_picked_ggnorm_none_p_kernel(tc, x_words, x_scales, w1, w2, w3, w4, offs
         e_out = {t: first_layer(q2, t, e_sb[t][:, :S], b, "e") for t, b in ((2, 4), (3, 5))}
 
         def gate(t, l):
-            nc.vector.tensor_tensor(u_sb[t][:, l, :], e_sb[t][:].indirect(lists[l][:]), y_sb[t][:], ALU.add)
+            parts = 2 if (t, l) == (0, 0) else 1
+            for a in range(parts):
+                cols = slice(a * S // parts, (a + 1) * S // parts)
+                nc.vector.tensor_tensor(u_sb[t][:, l, cols], e_sb[t][:].indirect(lists[l][:, cols.start // 16 : cols.stop // 16]), y_sb[t][:, cols], ALU.add)
             nc.scalar.activation(s_sb[t][l][:], u_sb[t][:, l, :], ACT.Sigmoid, scale=3.0)
 
         def w3_tile(t):
@@ -205,7 +208,7 @@ def tile_picked_ggnorm_none_p_kernel(tc, x_words, x_scales, w1, w2, w3, w4, offs
 
         zq = [(tile("z_bf%d" % c, [P, (b - a) * P * PACK], BF16), tile("z_codes%d" % c, [P, (b - a) * P], U32), tile("z_scales%d" % c, [P, (b - a) * P], U8)) for c, (a, b) in enumerate(STORES)]
         zt_pair = tile("zt_pair", [P, 2 * H], BF16)
-        zt = [zt_pair[:, :H], zt_pair[:, H:], zq[0][0][:, :H]]
+        zt = [zt_pair[:, :H], zt_pair[:, H:], tile("zt2", [P, H], BF16)[:]]
         root_last = zt_pair[:].bitcast(F32)
         staged_out = [tile("staged_out%d" % c, [P, TILES, (b - a) * P], F32) for c, (a, b) in enumerate(STORES)]
         num = [bank(jt, "num%d" % jt) for jt in range(last)]
@@ -221,7 +224,7 @@ def tile_picked_ggnorm_none_p_kernel(tc, x_words, x_scales, w1, w2, w3, w4, offs
             for u in range(2):
                 nc.tensor.transpose(back[:, u * P : (u + 1) * P], words[:, u * P : (u + 1) * P], ident[:])
             first = (jt - STORES[c][0]) * 2 * P
-            nc.scalar.copy(zq[c][0][:].bitcast(F32)[:, first : first + 2 * P].rearrange("p (j u) -> p j u", u=2), back[:, : 2 * P].rearrange("p (u j) -> p j u", u=2))
+            return lambda: nc.scalar.copy(zq[c][0][:].bitcast(F32)[:, first : first + 2 * P].rearrange("p (j u) -> p j u", u=2), back[:, : 2 * P].rearrange("p (u j) -> p j u", u=2))
 
         def last_layer(c, banks, copies):
             a, b = STORES[c]
@@ -239,7 +242,8 @@ def tile_picked_ggnorm_none_p_kernel(tc, x_words, x_scales, w1, w2, w3, w4, offs
         on_scalar = (nc.scalar.copy, nc.scalar.copy)
         for t in range(TILES):
             wide = tile("n_wide%d" % t, [P, 2, last * P], F32)
-            weigh(t, 0, last, [wide[:, l, :] for l in range(2)])
+            for a, b in ((0, last),) if t < last else ((0, last - 1), (last - 1, last)):
+                weigh(t, a, b, [wide[:, l, a * P : b * P] for l in range(2)])
             for jt in range(last):
                 add_turned(num[jt], t, [wide[:, l, jt * P : (jt + 1) * P] for l in range(2)])
 
@@ -248,23 +252,24 @@ def tile_picked_ggnorm_none_p_kernel(tc, x_words, x_scales, w1, w2, w3, w4, offs
         nc.scalar.activation(recip[:, :2, :], root[:, :2, :], ACT.Square)
         for t in range(TILES):
             weave(nc.scalar.copy, w4_raw, q4[t][0], t)
-        inverse_root(2)
-        nc.scalar.activation(recip_of[2], root[:, 2, :].rearrange("j (u c) -> j u c", u=2), ACT.Square)
         narrow = [recip[:, :, l * P : (l + 1) * P] for l in range(2)]
-        normalise(0, 0)
+        back_out = [normalise(0, 0), normalise(1, 0)]
         weigh(0, last, TILES, [narrow[l][:, 0, :] for l in range(2)])
-        normalise(1, 0)
         weigh(1, last, TILES, [narrow[l][:, 1, :] for l in range(2)])
+        quantize((w4_bf, w4_codes, w4_scales))
+        inverse_root(2)
+        back_out[0]()
+        nc.scalar.activation(recip_of[2], root[:, 2, :].rearrange("j (u c) -> j u c", u=2), ACT.Square)
+        back_out[1]()
         nc.scalar.activation(root_last, den[last][:], ACT.Abs_reciprocal_sqrt, bias=0.1)
         root_back = bank(last, "root_back")
         for t in range(TILES):
             nc.tensor.transpose(root_back[:, t * P : (t + 1) * P], root_last[:, t * P : (t + 1) * P], ident[:])
-        quantize((w4_bf, w4_codes, w4_scales))
+        normalise(2, 1)()
+        nc.scalar.activation(recip_last[:].rearrange("p (j t) -> p j t", t=TILES), root_back[:].rearrange("p (t j) -> p j t", t=TILES), ACT.Square)
         quantize(zq[0])
         last_layer(0, (TILES, TILES + 1), on_scalar)
         store(0, nc.sync, 0, TILES)
-        nc.scalar.activation(recip_last[:].rearrange("p (j t) -> p j t", t=TILES), root_back[:].rearrange("p (t j) -> p j t", t=TILES), ACT.Square)
-        normalise(2, 1)
         weigh(2, last, TILES, [narrow[l][:, 2, :] for l in range(2)])
         weigh(3, last, TILES, [narrow[l][:, 3, :] for l in range(2)])
         quantize(zq[1])

@@ -194,7 +194,7 @@ def tile_picked_ggnorm_none_p_kernel(tc, x_words, x_scales, w1, w2, w3, w4, offs
         recip = tile("recip", [P, TILES, H], F32)
         recip_of = [recip[:, 0, :].rearrange("j (u c) -> j u c", u=2), recip[:, 1, :].rearrange("j (u c) -> j u c", u=2), recip[:, 2:, : H // 2]]
         recip_last = tile("recip_last", [P, H], F32)
-        num_last = tile("num_last", [P, TILES, P], F32)
+        num_last = tile("num_last", [P, 2, P, 2], F32)
         last = TILES - 1
 
         def paired(ap):
@@ -277,12 +277,13 @@ def tile_picked_ggnorm_none_p_kernel(tc, x_words, x_scales, w1, w2, w3, w4, offs
         store(1, nc.sync, 0, TILES)
         halves = [slice(a * P // 2, (a + 1) * P // 2) for a in range(2)]
         for cols in halves:
-            nc.vector.tensor_tensor(num_last[:, :, cols], narrow[0][:, :, cols], narrow[1][:, :, cols], ALU.add)
+            terms = [narrow[l].rearrange("p (u e) j -> p u j e", u=2)[:, :, cols] for l in range(2)]
+            nc.vector.tensor_tensor(num_last[:, :, cols], terms[0], terms[1], ALU.add)
         for cols in halves:
             nc.vector.tensor_tensor(
-                zq[2][0][:].rearrange("p (j t) -> p j t", t=TILES)[:, cols],
-                num_last[:].rearrange("p t j -> p j t")[:, cols],
-                recip_last[:].rearrange("p (j t) -> p j t", t=TILES)[:, cols],
+                zq[2][0][:].rearrange("p (j u e) -> p j u e", u=2, e=2)[:, cols],
+                num_last[:].rearrange("p u j e -> p j u e")[:, cols],
+                recip_last[:].rearrange("p (j u e) -> p j u e", u=2, e=2)[:, cols],
                 ALU.mult,
             )
         for cols in halves:

from contextlib import ExitStack

import concourse.mybir as mybir
from concourse.masks import make_identity

K, T, S, N, H = 512, 2048, 512, 512, 512
FLOPS = 2 * (3 * K * H * S + H * N * S)

F32 = mybir.dt.float32
BF16 = mybir.dt.bfloat16
I32 = mybir.dt.int32
U32 = mybir.dt.uint32
U16 = mybir.dt.uint16
U8 = mybir.dt.uint8
FP8X4 = mybir.dt.float8_e4m3fn_x4
ACT = mybir.ActivationFunctionType
ALU = mybir.AluOpType

P = 128
PACK = 4
TILES = H // P
BLOCKS = 16
PER_BLOCK = P // BLOCKS
CHUNKS = ((0, 3), (3, 4))
STORES = ((0, 2), (2, 3), (3, 4))


def tile_picked_ggnorm_none_p_kernel(tc, x_words, x_scales, w1, w2, w3, w4, offs, p1, p2, out):
    nc = tc.nc
    with ExitStack() as ctx:
        sb = ctx.enter_context(tc.tile_pool(name="sb", bufs=1))
        psum = ctx.enter_context(tc.psum_pool(name="psum", bufs=1))

        def tile(name, shape, dtype):
            return sb.tile(shape, dtype, name=name, align_bytes=64)

        def bank(b, name):
            return psum.tile([P, 512], F32, name=name, tag="bank%d" % b)

        offs_sb = tile("offs_sb", [P, S // 16], U16)
        lists = [tile("p1_sb", [P, S // 16], U16), tile("p2_sb", [P, S // 16], U16)]
        xw_all = tile("xw_all", [P, T], I32)
        xs_all = tile("xs_all", [P, T], U8)
        xw = tile("xw", [P, S], U32)
        xs = tile("xs", [P, S], U8)
        w2_raw = tile("w2_raw", [P, PACK, H], F32)
        w1_raw = [tile("w1_raw%d" % a, [P, PACK, H // 2], F32) for a in range(2)]
        w3_raw = tile("w3_raw", [P, PACK, H], F32)
        w4_raw = tile("w4_raw", [P, PACK, N], F32)
        ident = tile("ident", [P, P], F32)
        warm = tile("warm", [P, 8], F32)

        def rows(w):
            return w.rearrange("(p j) c -> p j c", j=PACK)

        nc.gpsimd.memset(xs_all[:].bitcast(I32), 0)
        nc.vector.memset(warm[:, 0:1], 0.0)
        nc.scalar.activation(warm[:, 1:2], warm[:, 0:1], ACT.Sigmoid)
        nc.sync.dma_start(w2_raw[:], rows(w2))
        nc.sync.dma_start(offs_sb[:], offs)
        for q in range(4):
            nc.sync.dma_start(xs_all[32 * q : 32 * q + 4, :].bitcast(I32), x_scales[0, 4 * q : 4 * q + 4, :].bitcast(I32))
        nc.sync.dma_start(xw_all[:], x_words[0].rearrange("p c r -> p (c r)").bitcast(I32))
        for a in range(2):
            nc.sync.dma_start(w1_raw[a][:], rows(w1)[:, :, a * (H // 2) : (a + 1) * (H // 2)])
        nc.sync.dma_start(lists[0][:], p1)
        nc.sync.dma_start(lists[1][:], p2)
        nc.sync.dma_start(w3_raw[:], rows(w3))
        for t in range(TILES):
            nc.sync.dma_start(w4_raw[:, t, :], w4.rearrange("(b t r) n -> t b r n", t=TILES, r=PER_BLOCK)[t])

        make_identity(nc, ident[:])
        e_sb = [tile("e_sb%d" % t, [P, 2 * S], F32) for t in range(TILES)]
        for t in range(TILES):
            nc.gpsimd.memset(e_sb[t][:, S:], 0.0)
        y_sb = [tile("y_sb%d" % t, [P, S], F32) for t in range(TILES)]
        h_sb = [tile("h_sb%d" % t, [P, S], F32) for t in range(TILES)]
        u_sb = [tile("u_sb%d" % t, [P, 2, S], F32) for t in range(TILES)]
        s_sb = [[tile("s_sb%d_%d" % (t, l), [P, S], F32) for l in range(2)] for t in range(TILES)]

        def weight_tiles(name):
            return [
                (tile("%s_bf%d" % (name, t), [P, P * PACK], BF16), tile("%s_codes%d" % (name, t), [P, P], U32), tile("%s_scales%d" % (name, t), [P, P], U8))
                for t in range(TILES)
            ]

        q1, q2 = weight_tiles("w1"), weight_tiles("w2")
        w3_pairs = [(tile("w3_bf%d" % a, [P, 2 * P * PACK], BF16), tile("w3_codes%d" % a, [P, 2 * P], U32), tile("w3_scales%d" % a, [P, 2 * P], U8)) for a in range(TILES // 2)]
        q3 = [(bf[:, b * P * PACK : (b + 1) * P * PACK], codes[:, b * P : (b + 1) * P], scales[:, b * P : (b + 1) * P]) for bf, codes, scales in w3_pairs for b in range(2)]
        w4_bf = u_sb[TILES - 1][:].rearrange("p l s -> p (l s)").bitcast(BF16)
        w4_codes = tile("w4_codes", [P, N], U32)
        w4_scales = tile("w4_scales", [P, N], U8)
        q4 = [(w4_bf[:, t * P * PACK : (t + 1) * P * PACK], w4_codes[:, t * P : (t + 1) * P], w4_scales[:, t * P : (t + 1) * P]) for t in range(TILES)]

        def deal(copy, raw, staged, t, first_block, blocks):
            src = raw[:].rearrange("p j (b t r i) -> p t b r j i", t=TILES, r=PER_BLOCK // 4, i=4)[:, t]
            dst = staged[:].rearrange("p (b r i j) -> p b r j i", b=BLOCKS, i=4, j=PACK)[:, first_block : first_block + blocks]
            copy(dst, src)

        def weave(copy, raw, staged, t):
            src = raw[:, :, t * P : (t + 1) * P].rearrange("p j (c i) -> p c j i", i=4)
            dst = staged[:].rearrange("p (c i j) -> p c j i", i=4, j=PACK)
            copy(dst, src)

        def quantize(tiles):
            staged, codes, scales = tiles
            nc.vector.quantize_mx(out=codes[:].bitcast(FP8X4), scales=scales[:], in_=staged[:])

        def product(acc, weights, codes, scales):
            nc.tensor.matmul_mx(out=acc, lhsT=weights[1][:].bitcast(FP8X4), lhsT_scale=weights[2][:], rhs=codes.bitcast(FP8X4), rhs_scale=scales, start=True, stop=True)

        def first_layer(weights, t, dst, b, name):
            acc = bank(b, "%s_acc%d" % (name, t))
            product(acc[:], weights[t], xw[:], xs[:])
            return lambda: nc.scalar.copy(dst, acc[:])

        def add_turned(acc, t, pair):
            dst = acc[:, t * P : (t + 1) * P]
            for l in range(2):
                nc.tensor.matmul(dst, pair[l], ident[:], start=(l == 0), stop=(l == 1), is_transpose=True)

        nc.vector.tensor_copy(xs[:], xs_all[:].indirect(offs_sb[:]))
        for t in range(TILES + 1):
            if t < TILES:
                deal(nc.vector.tensor_copy, w2_raw, q2[t][0], t, 0, BLOCKS)
            if t > 0:
                quantize(q2[t - 1])
        nc.vector.tensor_copy(xw[:], xw_all[:].bitcast(U32).indirect(offs_sb[:]))
        for t in range(2):
            first_layer(q2, t, e_sb[t][:, :S], t, "e")()
        for t in range(TILES):
            deal(nc.vector.tensor_copy, w1_raw[0], q1[t][0], t, 0, BLOCKS // 2)
        for t in range(TILES + 1):
            if t < TILES:
                deal(nc.vector.tensor_copy, w1_raw[1], q1[t][0], t, BLOCKS // 2, BLOCKS // 2)
            if t > 0:
                quantize(q1[t - 1])
        for half, (b, copy) in enumerate(((4, nc.vector.tensor_copy), (5, nc.scalar.copy))):
            cols = slice(half * (S // 2), (half + 1) * (S // 2))
            acc = bank(b, "y_half%d" % half)
            product(acc[:, : S // 2], q1[0], xw[:, cols], xs[:, cols])
            copy(y_sb[0][:, cols], acc[:, : S // 2])
        y_out = {t: first_layer(q1, t, y_sb[t][:], b, "y") for t, b in ((1, 6), (2, 7), (3, 2))}
        e_out = {t: first_layer(q2, t, e_sb[t][:, :S], b, "e") for t, b in ((2, 4), (3, 5))}

        def gate(t, l):
            parts = 2 if (t, l) == (0, 0) else 1
            for a in range(parts):
                cols = slice(a * S // parts, (a + 1) * S // parts)
                nc.vector.tensor_tensor(u_sb[t][:, l, cols], e_sb[t][:].indirect(lists[l][:, cols.start // 16 : cols.stop // 16]), y_sb[t][:, cols], ALU.add)
            nc.scalar.activation(s_sb[t][l][:], u_sb[t][:, l, :], ACT.Sigmoid, scale=3.0)

        def w3_tile(t):
            deal(nc.scalar.copy, w3_raw, q3[t][0], t, 0, BLOCKS)
            if t % 2 == 1:
                quantize(w3_pairs[t // 2])

        def h_tile(t):
            first_layer(q3, t, h_sb[t][:], t, "h")()

        den = [bank(TILES + jt, "den%d" % jt) for jt in range(TILES)]

        def den_tile(t):
            for jt in range(TILES):
                add_turned(den[jt], t, [s_sb[t][l][:, jt * P : (jt + 1) * P] for l in range(2)])

        y_out[1]()
        w3_tile(0)
        e_out[2]()
        gate(0, 0)
        y_out[2]()
        w3_tile(1)
        gate(0, 1)
        e_out[3]()
        gate(1, 0)
        y_out[3]()
        w3_tile(2)
        gate(1, 1)
        den_tile(0)
        w3_tile(3)
        gate(2, 0)
        den_tile(1)
        h_tile(0)
        gate(2, 1)
        h_tile(1)
        den_tile(2)
        gate(3, 0)
        h_tile(2)
        gate(3, 1)
        den_tile(3)
        h_tile(3)

        root = tile("root", [P, TILES - 1, H], F32)
        recip = tile("recip", [P, TILES, H], F32)
        recip_of = [recip[:, 0, :].rearrange("j (u c) -> j u c", u=2), recip[:, 1, :].rearrange("j (u c) -> j u c", u=2), recip[:, 2:, : H // 2]]
        recip_last = tile("recip_last", [P, H], F32)
        num_last = tile("num_last", [P, 2, P, 2], F32)
        last = TILES - 1

        def paired(ap):
            return ap.rearrange("j (u e p) -> j u p e", u=2, e=2)

        def flat(ap):
            return ap.rearrange("j (u p e) -> j u p e", u=2, e=2)

        def inverse_root(jt):
            nc.scalar.activation(flat(root[:, jt, :]), paired(den[jt][:]), ACT.Abs_reciprocal_sqrt, bias=0.1)

        zq = [(tile("z_bf%d" % c, [P, (b - a) * P * PACK], BF16), tile("z_codes%d" % c, [P, (b - a) * P], U32), tile("z_scales%d" % c, [P, (b - a) * P], U8)) for c, (a, b) in enumerate(STORES)]
        zt_pair = tile("zt_pair", [P, 2 * H], BF16)
        zt = [zt_pair[:, :H], zt_pair[:, H:], tile("zt2", [P, H], BF16)[:]]
        root_last = zt_pair[:].bitcast(F32)
        staged_out = [tile("staged_out%d" % c, [P, TILES, (b - a) * P], F32) for c, (a, b) in enumerate(STORES)]
        num = [bank(jt, "num%d" % jt) for jt in range(last)]

        def weigh(t, a, b, pair):
            for l in range(2):
                nc.vector.tensor_tensor(pair[l], h_sb[t][:].indirect(lists[l][:, a * 8 : b * 8]), s_sb[t][l][:, a * P : b * P], ALU.mult)

        def normalise(jt, c):
            nc.vector.tensor_tensor(flat(zt[jt][:]), paired(num[jt][:]), recip_of[jt].rearrange("j u (p e) -> j u p e", e=2), ALU.mult)
            back = bank(TILES + jt, "back%d" % jt)
            words = zt[jt][:].bitcast(F32)
            for u in range(2):
                nc.tensor.transpose(back[:, u * P : (u + 1) * P], words[:, u * P : (u + 1) * P], ident[:])
            first = (jt - STORES[c][0]) * 2 * P
            return lambda: nc.scalar.copy(zq[c][0][:].bitcast(F32)[:, first : first + 2 * P].rearrange("p (j u) -> p j u", u=2), back[:, : 2 * P].rearrange("p (u j) -> p j u", u=2))

        def last_layer(c, banks, copies):
            a, b = STORES[c]
            width = (b - a) * P
            for half in range(2):
                acc = bank(banks[half], "out%d_%d" % (c, half))
                for m in range(2):
                    product(acc[:, m * width : (m + 1) * width], q4[2 * half + m], zq[c][1][:], zq[c][2][:])
                copies[half](staged_out[c][:, 2 * half : 2 * half + 2, :], acc[:, : 2 * width].rearrange("p (m j) -> p m j", m=2))

        def store(c, queue, m0, m1):
            a, b = STORES[c]
            queue.dma_start(out.rearrange("(m p) j -> p m j", p=P)[:, m0:m1, a * P : b * P], staged_out[c][:, m0:m1, :])

        on_scalar = (nc.scalar.copy, nc.scalar.copy)
        for t in range(TILES):
            wide = tile("n_wide%d" % t, [P, 2, last * P], F32)
            for a, b in ((0, last),) if t < last else ((0, last - 1), (last - 1, last)):
                weigh(t, a, b, [wide[:, l, a * P : b * P] for l in range(2)])
            for jt in range(last):
                add_turned(num[jt], t, [wide[:, l, jt * P : (jt + 1) * P] for l in range(2)])

        inverse_root(0)
        inverse_root(1)
        nc.scalar.activation(recip[:, :2, :], root[:, :2, :], ACT.Square)
        for t in range(TILES):
            weave(nc.scalar.copy, w4_raw, q4[t][0], t)
        narrow = [recip[:, :, l * P : (l + 1) * P] for l in range(2)]
        back_out = [normalise(0, 0), normalise(1, 0)]
        weigh(0, last, TILES, [narrow[l][:, 0, :] for l in range(2)])
        weigh(1, last, TILES, [narrow[l][:, 1, :] for l in range(2)])
        quantize((w4_bf, w4_codes, w4_scales))
        inverse_root(2)
        back_out[0]()
        nc.scalar.activation(recip_of[2], root[:, 2, :].rearrange("j (u c) -> j u c", u=2), ACT.Square)
        back_out[1]()
        nc.scalar.activation(root_last, den[last][:], ACT.Abs_reciprocal_sqrt, bias=0.1)
        root_back = bank(last, "root_back")
        for t in range(TILES):
            nc.tensor.transpose(root_back[:, t * P : (t + 1) * P], root_last[:, t * P : (t + 1) * P], ident[:])
        normalise(2, 1)()
        nc.scalar.activation(recip_last[:].rearrange("p (j t) -> p j t", t=TILES), root_back[:].rearrange("p (t j) -> p j t", t=TILES), ACT.Square)
        quantize(zq[0])
        last_layer(0, (TILES, TILES + 1), on_scalar)
        store(0, nc.sync, 0, TILES)
        weigh(2, last, TILES, [narrow[l][:, 2, :] for l in range(2)])
        weigh(3, last, TILES, [narrow[l][:, 3, :] for l in range(2)])
        quantize(zq[1])
        last_layer(1, (0, 1), on_scalar)
        store(1, nc.sync, 0, TILES)
        halves = [slice(a * P // 2, (a + 1) * P // 2) for a in range(2)]
        for cols in halves:
            terms = [narrow[l].rearrange("p (u e) j -> p u j e", u=2)[:, :, cols] for l in range(2)]
            nc.vector.tensor_tensor(num_last[:, :, cols], terms[0], terms[1], ALU.add)
        for cols in halves:
            nc.vector.tensor_tensor(
                zq[2][0][:].rearrange("p (j u e) -> p j u e", u=2, e=2)[:, cols],
                num_last[:].rearrange("p u j e -> p j u e")[:, cols],
                recip_last[:].rearrange("p (j u e) -> p j u e", u=2, e=2)[:, cols],
                ALU.mult,
            )
        for cols in halves:
            quantize((zq[2][0][:, cols.start * PACK : cols.stop * PACK], zq[2][1][:, cols], zq[2][2][:, cols]))
        last_layer(2, (2, last), (nc.vector.tensor_copy, nc.scalar.copy))
        store(2, nc.sync, 0, 2)
        store(2, nc.scalar, 2, TILES)
